import numpy as np, ml_dtypes
CORES = [3,11,19,27,35,43,131,139,147,155,163,171]
N = 12
G1 = [0,1,2,3,4,5,6,7,8,9,10,11]
G2 = [0,1,2,3,4,5]
G3 = [6,7,8,9,10,11]
ROOT3 = 2
def setup_inputs(rng):
    return {"x1": rng.standard_normal((N, 128, 120), dtype=np.float32).astype(ml_dtypes.bfloat16), "x2": rng.standard_normal((N, 128, 2), dtype=np.float32), "x3": rng.standard_normal((N, 128, 4), dtype=np.float32)}
def reference(x1, x2, x3):
    out = {}
    y = np.full((N, 128, 120), np.nan, x1.dtype)
    for i, r in enumerate(G1):
        y[r] = np.concatenate([x1[s][:, 10 * i:10 * i + 10] for s in G1], axis=1)
    out["y1"] = y
    y = np.full((N, 128, 2), np.nan, x2.dtype)
    s = x2[G2].max(axis=0)
    for r in G2:
        y[r] = s
    out["y2"] = y
    y = np.full((N, 128, 24), np.nan, x3.dtype)
    y[G3[ROOT3]] = np.concatenate([x3[r] for r in G3], axis=1)
    out["y3"] = y
    return out

@@ -1,0 +1,172 @@
+from concourse.bass import DstId, RemoteDMATransfer
+
+BLK = 10
+PAD = 5
+W2 = 2
+W3 = 4
+LANES = 4
+
+SCRATCH = {
+    "s1": ("sbuf", [128, 120], "bfloat16"),
+    "land1": ("sbuf", [128, 120], "bfloat16"),
+    "s3": ("sbuf", [128, W3], "float32"),
+    "land3": ("sbuf", [128, 24], "float32"),
+    "z": ("sbuf", [128, PAD - W2], "float32"),
+    "d2": ("dram", [128, PAD], "float32"),
+    "g2": ("dram", [6, 128, PAD], "float32"),
+    "r2": ("dram", [128, PAD], "float32"),
+}
+SEMAPHORES = ["fill", "ld1", "ldx", "got1", "arr1", "arr2", "res2", "arr3", "sent", "st"]
+
+
+def _bits(mask):
+    return [b for b in range(mask.bit_length()) if (mask >> b) & 1]
+
+
+def _pack(engines):
+    m = 0
+    for b in engines:
+        m |= 1 << b
+    return m
+
+
+def _common(topo, src, dsts):
+    m = topo.mask(src, dsts[0])
+    for d in dsts[1:]:
+        m &= topo.mask(src, d)
+    return _bits(m)
+
+
+def _dst(topo, dst, src):
+    rid, pid = topo.addr(dst, src)
+    return DstId(rid=rid, pnc=pid)
+
+
+def _way(topo, a, b):
+    return 1 if (topo.mates(a, b) or topo.same_plane(a, b)) else 2
+
+
+def _team(T, topo, i):
+    g1 = T.tables["G1"]
+    me = T.cores[g1[i]]
+    world = range((max(topo.host(c) for c in T.cores) + 1) * topo.CORES_PER_HOST)
+    idle = [c for c in world if c != me and topo.host(c) == topo.host(me) and topo.chip(c) == topo.chip(me)
+            and topo.die(c) == topo.die(me)]
+    others = [j for j in range(len(g1)) if j != i]
+    core_of = dict((j, T.cores[g1[j]]) for j in others)
+    wide = [c for c in idle if all(topo.may_write(c, core_of[j]) for j in others)][0]
+    narrow = [c for c in idle if c != wide]
+    plane, fold = narrow[0], narrow[1]
+    by_plane = [j for j in others if topo.may_write(plane, core_of[j])][:LANES]
+    rest = sorted([j for j in others if j not in by_plane], key=lambda j: _way(topo, me, core_of[j]))
+    return {"me": me, "wide": wide, "plane": plane, "fold": fold,
+            "jobs": {plane: by_plane, wide: rest[:LANES], me: rest[LANES:]}}
+
+
+def _lane_width(T, topo, sender, members):
+    g1 = T.tables["G1"]
+    return len(_common(topo, sender, [T.cores[g1[j]] for j in members])) // LANES
+
+
+def _send_blocks(g, T, topo, core, i, members, extra):
+    g1 = T.tables["G1"]
+    engines = _common(topo, core, [T.cores[g1[j]] for j in members])
+    per = len(engines) // LANES
+    trs = []
+    for k, j in enumerate(members):
+        trs.append(RemoteDMATransfer(
+            dst_ids=[_dst(topo, T.cores[g1[j]], core)], dma_engine_mask=_pack(engines[k * per:(k + 1) * per]),
+            remote_sem=T.sem.arr1, src=T.s1[:, BLK * j:BLK * (j + 1)], dst=T.land1[:, BLK * i:BLK * (i + 1)]))
+    if extra is not None:
+        dsts, src, dst, sem = extra
+        k = len(members)
+        trs.append(RemoteDMATransfer(
+            dst_ids=[_dst(topo, d, core) for d in dsts], dma_engine_mask=_pack(engines[k * per:(k + 1) * per]),
+            remote_sem=sem, srcs=[src], dsts=[dst for d in dsts]))
+    g.remote_dma_fused(trs, local_sem=T.sem.sent)
+    return per * len(trs)
+
+
+def rank_program(g, core, T, topo):
+    g1, g2, g3 = T.tables["G1"], T.tables["G2"], T.tables["G3"]
+    root3 = g3[T.tables["ROOT3"]]
+    teams = [_team(T, topo, i) for i in range(len(g1))]
+    member_of = dict((r, i) for i, r in enumerate(g1))
+    folds = [teams[member_of[r]]["fold"] for r in g2]
+    rank = T.rank_of(core)
+
+    if rank is None:
+        for i, t in enumerate(teams):
+            if core in (t["wide"], t["plane"]):
+                g.wait_ge(T.sem.got1, len(_common(topo, t["me"], [t["wide"], t["plane"]])))
+                n = _send_blocks(g, T, topo, core, i, t["jobs"][core], None)
+                g.wait_ge(T.sem.sent, n)
+            elif core == t["fold"] and g1[i] in g2:
+                n_in = sum(_lane_width(T, topo, T.cores[r], teams[member_of[r]]["jobs"][T.cores[r]]) for r in g2)
+                g.wait_ge(T.sem.arr2, n_in)
+                engines = _common(topo, core, [t["me"]])
+                g.remote_dma_fused([RemoteDMATransfer(
+                    dst_ids=[_dst(topo, t["me"], core)], dma_engine_mask=_pack(engines), remote_sem=T.sem.res2,
+                    srcs=[T.g2[k] for k in range(len(g2))], dsts=[T.r2[:]], alu_op=2)], local_sem=T.sem.sent)
+                g.wait_ge(T.sem.sent, len(engines))
+        return
+
+    i = member_of[rank]
+    t = teams[i]
+    own = slice(BLK * i, BLK * (i + 1))
+
+    g.sync.dma_start(T.s1[:], T.x1[:]).then_inc(T.sem.ld1, 16)
+    g.sync.dma_start(T.land1[:, own], T.x1[:, own]).then_inc(T.sem.arr1, 16)
+    if rank in g2:
+        g.vector.memset(T.z[:], 0.0).then_inc(T.sem.fill, 1)
+        g.scalar.dma_start(T.d2[:, 0:W2], T.x2[:]).then_inc(T.sem.ldx, 16)
+        g.scalar.wait_ge(T.sem.fill, 1)
+        g.scalar.dma_start(T.d2[:, W2:PAD], T.z[:]).then_inc(T.sem.ldx, 16)
+    elif rank == root3:
+        k = g3.index(rank)
+        g.scalar.dma_start(T.land3[:, W3 * k:W3 * (k + 1)], T.x3[:]).then_inc(T.sem.arr3, 16)
+    elif rank in g3:
+        g.scalar.dma_start(T.s3[:], T.x3[:]).then_inc(T.sem.ldx, 16)
+
+    helpers = [t["wide"], t["plane"]]
+    engines = _common(topo, core, helpers)
+    g.wait_ge(T.sem.ld1, 16)
+    g.remote_dma_fused([RemoteDMATransfer(
+        dst_ids=[_dst(topo, h, core) for h in helpers], dma_engine_mask=_pack(engines), remote_sem=T.sem.got1,
+        srcs=[T.s1[:]], dsts=[T.s1[:] for h in helpers])], local_sem=T.sem.sent)
+    sent = len(engines)
+
+    extra = None
+    if rank in g2:
+        g.wait_ge(T.sem.ldx, 32)
+        extra = (folds, T.d2[:], T.g2[g2.index(rank)], T.sem.arr2)
+    sent += _send_blocks(g, T, topo, core, i, t["jobs"][core], extra)
+
+    if rank in g3 and rank != root3:
+        k = g3.index(rank)
+        dst = T.cores[root3]
+        engines = _common(topo, core, [dst])
+        rid, pid = topo.addr(dst, core)
+        g.wait_ge(T.sem.ldx, 16)
+        g.remote_dma(T.land3[:, W3 * k:W3 * (k + 1)], T.s3[:], T.sem.arr3, T.sem.sent, pid, rid, _pack(engines))
+        sent += len(engines)
+
+    n1 = 16
+    for j, u in enumerate(teams):
+        for sender, members in u["jobs"].items():
+            if i in members:
+                n1 += _lane_width(T, topo, sender, members)
+    g.sync.wait_ge(T.sem.arr1, n1)
+    g.sync.dma_start(T.y1[:], T.land1[:]).then_inc(T.sem.st, 16)
+    stores = 1
+    if rank in g2:
+        g.scalar.wait_ge(T.sem.res2, len(_common(topo, t["fold"], [core])))
+        g.scalar.dma_start(T.y2[:], T.r2[:, 0:W2]).then_inc(T.sem.st, 16)
+        stores += 1
+    elif rank == root3:
+        n3 = 16 + sum(len(_common(topo, T.cores[r], [core])) for r in g3 if r != rank)
+        g.scalar.wait_ge(T.sem.arr3, n3)
+        g.scalar.dma_start(T.y3[:], T.land3[:]).then_inc(T.sem.st, 16)
+        stores += 1
+    g.wait_ge(T.sem.sent, sent)
+    g.wait_ge(T.sem.st, 16 * stores)

@@ -1,7 +1,6 @@
 from concourse.bass import DstId, RemoteDMATransfer
 
 BLK = 10
-PAD = 5
 W2 = 2
 W3 = 4
 LANES = 4
@@ -11,12 +10,11 @@ SCRATCH = {
     "land1": ("sbuf", [128, 120], "bfloat16"),
     "s3": ("sbuf", [128, W3], "float32"),
     "land3": ("sbuf", [128, 24], "float32"),
-    "z": ("sbuf", [128, PAD - W2], "float32"),
-    "d2": ("dram", [128, PAD], "float32"),
-    "g2": ("dram", [6, 128, PAD], "float32"),
-    "r2": ("dram", [128, PAD], "float32"),
+    "d2": ("dram", [128, W2], "float32"),
+    "g2": ("dram", [6, 128, W2], "float32"),
+    "r2": ("dram", [128, W2], "float32"),
 }
-SEMAPHORES = ["fill", "ld1", "ldx", "got1", "arr1", "arr2", "res2", "arr3", "sent", "st"]
+SEMAPHORES = ["ld1", "ldx", "got1", "arr1", "arr2", "res2", "arr3", "sent", "st"]
 
 
 def _bits(mask):
@@ -68,7 +66,7 @@ def _lane_width(T, topo, sender, members):
     return len(_common(topo, sender, [T.cores[g1[j]] for j in members])) // LANES
 
 
-def _send_blocks(g, T, topo, core, i, members, extra):
+def _send_blocks(g, T, topo, core, i, members):
     g1 = T.tables["G1"]
     engines = _common(topo, core, [T.cores[g1[j]] for j in members])
     per = len(engines) // LANES
@@ -77,12 +75,6 @@ def _send_blocks(g, T, topo, core, i, members, extra):
         trs.append(RemoteDMATransfer(
             dst_ids=[_dst(topo, T.cores[g1[j]], core)], dma_engine_mask=_pack(engines[k * per:(k + 1) * per]),
             remote_sem=T.sem.arr1, src=T.s1[:, BLK * j:BLK * (j + 1)], dst=T.land1[:, BLK * i:BLK * (i + 1)]))
-    if extra is not None:
-        dsts, src, dst, sem = extra
-        k = len(members)
-        trs.append(RemoteDMATransfer(
-            dst_ids=[_dst(topo, d, core) for d in dsts], dma_engine_mask=_pack(engines[k * per:(k + 1) * per]),
-            remote_sem=sem, srcs=[src], dsts=[dst for d in dsts]))
     g.remote_dma_fused(trs, local_sem=T.sem.sent)
     return per * len(trs)
 
@@ -99,11 +91,10 @@ def rank_program(g, core, T, topo):
         for i, t in enumerate(teams):
             if core in (t["wide"], t["plane"]):
                 g.wait_ge(T.sem.got1, len(_common(topo, t["me"], [t["wide"], t["plane"]])))
-                n = _send_blocks(g, T, topo, core, i, t["jobs"][core], None)
+                n = _send_blocks(g, T, topo, core, i, t["jobs"][core])
                 g.wait_ge(T.sem.sent, n)
             elif core == t["fold"] and g1[i] in g2:
-                n_in = sum(_lane_width(T, topo, T.cores[r], teams[member_of[r]]["jobs"][T.cores[r]]) for r in g2)
-                g.wait_ge(T.sem.arr2, n_in)
+                g.wait_ge(T.sem.arr2, sum(len(_common(topo, T.cores[r], folds)) for r in g2))
                 engines = _common(topo, core, [t["me"]])
                 g.remote_dma_fused([RemoteDMATransfer(
                     dst_ids=[_dst(topo, t["me"], core)], dma_engine_mask=_pack(engines), remote_sem=T.sem.res2,
@@ -116,17 +107,14 @@ def rank_program(g, core, T, topo):
     own = slice(BLK * i, BLK * (i + 1))
 
     g.sync.dma_start(T.s1[:], T.x1[:]).then_inc(T.sem.ld1, 16)
-    g.sync.dma_start(T.land1[:, own], T.x1[:, own]).then_inc(T.sem.arr1, 16)
     if rank in g2:
-        g.vector.memset(T.z[:], 0.0).then_inc(T.sem.fill, 1)
-        g.scalar.dma_start(T.d2[:, 0:W2], T.x2[:]).then_inc(T.sem.ldx, 16)
-        g.scalar.wait_ge(T.sem.fill, 1)
-        g.scalar.dma_start(T.d2[:, W2:PAD], T.z[:]).then_inc(T.sem.ldx, 16)
+        g.sync.dma_start(T.d2[:], T.x2[:]).then_inc(T.sem.ldx, 16)
     elif rank == root3:
         k = g3.index(rank)
-        g.scalar.dma_start(T.land3[:, W3 * k:W3 * (k + 1)], T.x3[:]).then_inc(T.sem.arr3, 16)
+        g.sync.dma_start(T.land3[:, W3 * k:W3 * (k + 1)], T.x3[:]).then_inc(T.sem.arr3, 16)
     elif rank in g3:
-        g.scalar.dma_start(T.s3[:], T.x3[:]).then_inc(T.sem.ldx, 16)
+        g.sync.dma_start(T.s3[:], T.x3[:]).then_inc(T.sem.ldx, 16)
+    g.sync.dma_start(T.land1[:, own], T.x1[:, own]).then_inc(T.sem.arr1, 16)
 
     helpers = [t["wide"], t["plane"]]
     engines = _common(topo, core, helpers)
@@ -136,11 +124,15 @@ def rank_program(g, core, T, topo):
         srcs=[T.s1[:]], dsts=[T.s1[:] for h in helpers])], local_sem=T.sem.sent)
     sent = len(engines)
 
-    extra = None
     if rank in g2:
-        g.wait_ge(T.sem.ldx, 32)
-        extra = (folds, T.d2[:], T.g2[g2.index(rank)], T.sem.arr2)
-    sent += _send_blocks(g, T, topo, core, i, t["jobs"][core], extra)
+        engines = _common(topo, core, folds)
+        g.wait_ge(T.sem.ldx, 16)
+        g.remote_dma_fused([RemoteDMATransfer(
+            dst_ids=[_dst(topo, f, core) for f in folds], dma_engine_mask=_pack(engines), remote_sem=T.sem.arr2,
+            srcs=[T.d2[:]], dsts=[T.g2[g2.index(rank)] for f in folds])], local_sem=T.sem.sent)
+        sent += len(engines)
+
+    sent += _send_blocks(g, T, topo, core, i, t["jobs"][core])
 
     if rank in g3 and rank != root3:
         k = g3.index(rank)
@@ -152,7 +144,7 @@ def rank_program(g, core, T, topo):
         sent += len(engines)
 
     n1 = 16
-    for j, u in enumerate(teams):
+    for u in teams:
         for sender, members in u["jobs"].items():
             if i in members:
                 n1 += _lane_width(T, topo, sender, members)
@@ -161,7 +153,7 @@ def rank_program(g, core, T, topo):
     stores = 1
     if rank in g2:
         g.scalar.wait_ge(T.sem.res2, len(_common(topo, t["fold"], [core])))
-        g.scalar.dma_start(T.y2[:], T.r2[:, 0:W2]).then_inc(T.sem.st, 16)
+        g.scalar.dma_start(T.y2[:], T.r2[:]).then_inc(T.sem.st, 16)
         stores += 1
     elif rank == root3:
         n3 = 16 + sum(len(_common(topo, T.cores[r], [core])) for r in g3 if r != rank)

@@ -57,23 +57,25 @@ def _team(T, topo, i):
     plane, fold = narrow[0], narrow[1]
     by_plane = [j for j in others if topo.may_write(plane, core_of[j])][:LANES]
     rest = sorted([j for j in others if j not in by_plane], key=lambda j: _way(topo, me, core_of[j]))
+    half = LANES // 2
     return {"me": me, "wide": wide, "plane": plane, "fold": fold,
-            "jobs": {plane: by_plane, wide: rest[:LANES], me: rest[LANES:]}}
+            "calls": [(plane, by_plane, LANES), (wide, rest[half:LANES], half), (wide, rest[:half], half),
+                      (me, rest[LANES:], LANES)]}
 
 
-def _lane_width(T, topo, sender, members):
+def _lane_width(T, topo, sender, members, lanes):
     g1 = T.tables["G1"]
-    return len(_common(topo, sender, [T.cores[g1[j]] for j in members])) // LANES
+    return len(_common(topo, sender, [T.cores[g1[j]] for j in members])) // lanes
 
 
-def _send_blocks(g, T, topo, core, i, members):
+def _send_blocks(g, T, topo, i, sender, members, lanes):
     g1 = T.tables["G1"]
-    engines = _common(topo, core, [T.cores[g1[j]] for j in members])
-    per = len(engines) // LANES
+    engines = _common(topo, sender, [T.cores[g1[j]] for j in members])
+    per = len(engines) // lanes
     trs = []
     for k, j in enumerate(members):
         trs.append(RemoteDMATransfer(
-            dst_ids=[_dst(topo, T.cores[g1[j]], core)], dma_engine_mask=_pack(engines[k * per:(k + 1) * per]),
+            dst_ids=[_dst(topo, T.cores[g1[j]], sender)], dma_engine_mask=_pack(engines[k * per:(k + 1) * per]),
             remote_sem=T.sem.arr1, src=T.s1[:, BLK * j:BLK * (j + 1)], dst=T.land1[:, BLK * i:BLK * (i + 1)]))
     g.remote_dma_fused(trs, local_sem=T.sem.sent)
     return per * len(trs)
@@ -91,7 +93,10 @@ def rank_program(g, core, T, topo):
         for i, t in enumerate(teams):
             if core in (t["wide"], t["plane"]):
                 g.wait_ge(T.sem.got1, len(_common(topo, t["me"], [t["wide"], t["plane"]])))
-                n = _send_blocks(g, T, topo, core, i, t["jobs"][core])
+                n = 0
+                for call in t["calls"]:
+                    if call[0] == core:
+                        n += _send_blocks(g, T, topo, i, *call)
                 g.wait_ge(T.sem.sent, n)
             elif core == t["fold"] and g1[i] in g2:
                 g.wait_ge(T.sem.arr2, sum(len(_common(topo, T.cores[r], folds)) for r in g2))
@@ -132,7 +137,9 @@ def rank_program(g, core, T, topo):
             srcs=[T.d2[:]], dsts=[T.g2[g2.index(rank)] for f in folds])], local_sem=T.sem.sent)
         sent += len(engines)
 
-    sent += _send_blocks(g, T, topo, core, i, t["jobs"][core])
+    for call in t["calls"]:
+        if call[0] == core:
+            sent += _send_blocks(g, T, topo, i, *call)
 
     if rank in g3 and rank != root3:
         k = g3.index(rank)
@@ -145,9 +152,9 @@ def rank_program(g, core, T, topo):
 
     n1 = 16
     for u in teams:
-        for sender, members in u["jobs"].items():
-            if i in members:
-                n1 += _lane_width(T, topo, sender, members)
+        for call in u["calls"]:
+            if i in call[1]:
+                n1 += _lane_width(T, topo, *call)
     g.sync.wait_ge(T.sem.arr1, n1)
     g.sync.dma_start(T.y1[:], T.land1[:]).then_inc(T.sem.st, 16)
     stores = 1

@@ -56,29 +56,36 @@ def _team(T, topo, i):
     narrow = [c for c in idle if c != wide]
     plane, fold = narrow[0], narrow[1]
     by_plane = [j for j in others if topo.may_write(plane, core_of[j])][:LANES]
-    rest = sorted([j for j in others if j not in by_plane], key=lambda j: _way(topo, me, core_of[j]))
-    half = LANES // 2
+    rest = sorted([j for j in others if j not in by_plane], key=lambda j: -_way(topo, me, core_of[j]))
+    mine, by_wide = rest[:LANES], rest[LANES:]
     return {"me": me, "wide": wide, "plane": plane, "fold": fold,
-            "calls": [(plane, by_plane, LANES), (wide, rest[half:LANES], half), (wide, rest[:half], half),
-                      (me, rest[LANES:], LANES)]}
+            "calls": [(plane, by_plane, [LANES] * len(by_plane)),
+                      (wide, by_wide[:1], [1]),
+                      (wide, by_wide[1:], [len(by_wide) - 1] * (len(by_wide) - 1)),
+                      (me, mine, [LANES] * len(mine))]}
 
 
-def _lane_width(T, topo, sender, members, lanes):
-    g1 = T.tables["G1"]
-    return len(_common(topo, sender, [T.cores[g1[j]] for j in members])) // lanes
-
-
-def _send_blocks(g, T, topo, i, sender, members, lanes):
+def _lanes(T, topo, sender, members, parts):
     g1 = T.tables["G1"]
     engines = _common(topo, sender, [T.cores[g1[j]] for j in members])
-    per = len(engines) // lanes
+    out = []
+    at = 0
+    for p in parts:
+        out.append(engines[at:at + len(engines) // p])
+        at += len(engines) // p
+    return out
+
+
+def _send_blocks(g, T, topo, i, sender, members, parts):
+    g1 = T.tables["G1"]
+    lanes = _lanes(T, topo, sender, members, parts)
     trs = []
-    for k, j in enumerate(members):
+    for j, lane in zip(members, lanes):
         trs.append(RemoteDMATransfer(
-            dst_ids=[_dst(topo, T.cores[g1[j]], sender)], dma_engine_mask=_pack(engines[k * per:(k + 1) * per]),
+            dst_ids=[_dst(topo, T.cores[g1[j]], sender)], dma_engine_mask=_pack(lane),
             remote_sem=T.sem.arr1, src=T.s1[:, BLK * j:BLK * (j + 1)], dst=T.land1[:, BLK * i:BLK * (i + 1)]))
     g.remote_dma_fused(trs, local_sem=T.sem.sent)
-    return per * len(trs)
+    return sum(len(lane) for lane in lanes)
 
 
 def rank_program(g, core, T, topo):
@@ -121,7 +128,7 @@ def rank_program(g, core, T, topo):
         g.sync.dma_start(T.s3[:], T.x3[:]).then_inc(T.sem.ldx, 16)
     g.sync.dma_start(T.land1[:, own], T.x1[:, own]).then_inc(T.sem.arr1, 16)
 
-    helpers = [t["wide"], t["plane"]]
+    helpers = [t["plane"], t["wide"]]
     engines = _common(topo, core, helpers)
     g.wait_ge(T.sem.ld1, 16)
     g.remote_dma_fused([RemoteDMATransfer(
@@ -154,7 +161,7 @@ def rank_program(g, core, T, topo):
     for u in teams:
         for call in u["calls"]:
             if i in call[1]:
-                n1 += _lane_width(T, topo, *call)
+                n1 += len(_lanes(T, topo, *call)[call[1].index(i)])
     g.sync.wait_ge(T.sem.arr1, n1)
     g.sync.dma_start(T.y1[:], T.land1[:]).then_inc(T.sem.st, 16)
     stores = 1

from concourse.bass import DstId, RemoteDMATransfer

BLK = 10
W2 = 2
W3 = 4
LANES = 4

SCRATCH = {
    "s1": ("sbuf", [128, 120], "bfloat16"),
    "land1": ("sbuf", [128, 120], "bfloat16"),
    "s3": ("sbuf", [128, W3], "float32"),
    "land3": ("sbuf", [128, 24], "float32"),
    "d2": ("dram", [128, W2], "float32"),
    "g2": ("dram", [6, 128, W2], "float32"),
    "r2": ("dram", [128, W2], "float32"),
}
SEMAPHORES = ["ld1", "ldx", "got1", "arr1", "arr2", "res2", "arr3", "sent", "st"]


def _bits(mask):
    return [b for b in range(mask.bit_length()) if (mask >> b) & 1]


def _pack(engines):
    m = 0
    for b in engines:
        m |= 1 << b
    return m


def _common(topo, src, dsts):
    m = topo.mask(src, dsts[0])
    for d in dsts[1:]:
        m &= topo.mask(src, d)
    return _bits(m)


def _dst(topo, dst, src):
    rid, pid = topo.addr(dst, src)
    return DstId(rid=rid, pnc=pid)


def _way(topo, a, b):
    return 1 if (topo.mates(a, b) or topo.same_plane(a, b)) else 2


def _team(T, topo, i):
    g1 = T.tables["G1"]
    me = T.cores[g1[i]]
    world = range((max(topo.host(c) for c in T.cores) + 1) * topo.CORES_PER_HOST)
    idle = [c for c in world if c != me and topo.host(c) == topo.host(me) and topo.chip(c) == topo.chip(me)
            and topo.die(c) == topo.die(me)]
    others = [j for j in range(len(g1)) if j != i]
    core_of = dict((j, T.cores[g1[j]]) for j in others)
    wide = [c for c in idle if all(topo.may_write(c, core_of[j]) for j in others)][0]
    narrow = [c for c in idle if c != wide]
    plane, fold = narrow[0], narrow[1]
    by_plane = [j for j in others if topo.may_write(plane, core_of[j])][:LANES]
    rest = sorted([j for j in others if j not in by_plane], key=lambda j: -_way(topo, me, core_of[j]))
    mine, by_wide = rest[:LANES], rest[LANES:]
    return {"me": me, "wide": wide, "plane": plane, "fold": fold,
            "calls": [(plane, by_plane, [LANES] * len(by_plane)),
                      (wide, by_wide[:1], [1]),
                      (wide, by_wide[1:], [len(by_wide) - 1] * (len(by_wide) - 1)),
                      (me, mine, [LANES] * len(mine))]}


def _lanes(T, topo, sender, members, parts):
    g1 = T.tables["G1"]
    engines = _common(topo, sender, [T.cores[g1[j]] for j in members])
    out = []
    at = 0
    for p in parts:
        out.append(engines[at:at + len(engines) // p])
        at += len(engines) // p
    return out


def _send_blocks(g, T, topo, i, sender, members, parts):
    g1 = T.tables["G1"]
    lanes = _lanes(T, topo, sender, members, parts)
    trs = []
    for j, lane in zip(members, lanes):
        trs.append(RemoteDMATransfer(
            dst_ids=[_dst(topo, T.cores[g1[j]], sender)], dma_engine_mask=_pack(lane),
            remote_sem=T.sem.arr1, src=T.s1[:, BLK * j:BLK * (j + 1)], dst=T.land1[:, BLK * i:BLK * (i + 1)]))
    g.remote_dma_fused(trs, local_sem=T.sem.sent)
    return sum(len(lane) for lane in lanes)


def rank_program(g, core, T, topo):
    g1, g2, g3 = T.tables["G1"], T.tables["G2"], T.tables["G3"]
    root3 = g3[T.tables["ROOT3"]]
    teams = [_team(T, topo, i) for i in range(len(g1))]
    member_of = dict((r, i) for i, r in enumerate(g1))
    folds = [teams[member_of[r]]["fold"] for r in g2]
    rank = T.rank_of(core)

    if rank is None:
        for i, t in enumerate(teams):
            if core in (t["wide"], t["plane"]):
                g.wait_ge(T.sem.got1, len(_common(topo, t["me"], [t["wide"], t["plane"]])))
                n = 0
                for call in t["calls"]:
                    if call[0] == core:
                        n += _send_blocks(g, T, topo, i, *call)
                g.wait_ge(T.sem.sent, n)
            elif core == t["fold"] and g1[i] in g2:
                g.wait_ge(T.sem.arr2, sum(len(_common(topo, T.cores[r], folds)) for r in g2))
                engines = _common(topo, core, [t["me"]])
                g.remote_dma_fused([RemoteDMATransfer(
                    dst_ids=[_dst(topo, t["me"], core)], dma_engine_mask=_pack(engines), remote_sem=T.sem.res2,
                    srcs=[T.g2[k] for k in range(len(g2))], dsts=[T.r2[:]], alu_op=2)], local_sem=T.sem.sent)
                g.wait_ge(T.sem.sent, len(engines))
        return

    i = member_of[rank]
    t = teams[i]
    own = slice(BLK * i, BLK * (i + 1))

    g.sync.dma_start(T.s1[:], T.x1[:]).then_inc(T.sem.ld1, 16)
    if rank in g2:
        g.sync.dma_start(T.d2[:], T.x2[:]).then_inc(T.sem.ldx, 16)
    elif rank == root3:
        k = g3.index(rank)
        g.sync.dma_start(T.land3[:, W3 * k:W3 * (k + 1)], T.x3[:]).then_inc(T.sem.arr3, 16)
    elif rank in g3:
        g.sync.dma_start(T.s3[:], T.x3[:]).then_inc(T.sem.ldx, 16)
    g.sync.dma_start(T.land1[:, own], T.x1[:, own]).then_inc(T.sem.arr1, 16)

    helpers = [t["plane"], t["wide"]]
    engines = _common(topo, core, helpers)
    g.wait_ge(T.sem.ld1, 16)
    g.remote_dma_fused([RemoteDMATransfer(
        dst_ids=[_dst(topo, h, core) for h in helpers], dma_engine_mask=_pack(engines), remote_sem=T.sem.got1,
        srcs=[T.s1[:]], dsts=[T.s1[:] for h in helpers])], local_sem=T.sem.sent)
    sent = len(engines)

    if rank in g2:
        engines = _common(topo, core, folds)
        g.wait_ge(T.sem.ldx, 16)
        g.remote_dma_fused([RemoteDMATransfer(
            dst_ids=[_dst(topo, f, core) for f in folds], dma_engine_mask=_pack(engines), remote_sem=T.sem.arr2,
            srcs=[T.d2[:]], dsts=[T.g2[g2.index(rank)] for f in folds])], local_sem=T.sem.sent)
        sent += len(engines)

    for call in t["calls"]:
        if call[0] == core:
            sent += _send_blocks(g, T, topo, i, *call)

    if rank in g3 and rank != root3:
        k = g3.index(rank)
        dst = T.cores[root3]
        engines = _common(topo, core, [dst])
        rid, pid = topo.addr(dst, core)
        g.wait_ge(T.sem.ldx, 16)
        g.remote_dma(T.land3[:, W3 * k:W3 * (k + 1)], T.s3[:], T.sem.arr3, T.sem.sent, pid, rid, _pack(engines))
        sent += len(engines)

    n1 = 16
    for u in teams:
        for call in u["calls"]:
            if i in call[1]:
                n1 += len(_lanes(T, topo, *call)[call[1].index(i)])
    g.sync.wait_ge(T.sem.arr1, n1)
    g.sync.dma_start(T.y1[:], T.land1[:]).then_inc(T.sem.st, 16)
    stores = 1
    if rank in g2:
        g.scalar.wait_ge(T.sem.res2, len(_common(topo, t["fold"], [core])))
        g.scalar.dma_start(T.y2[:], T.r2[:]).then_inc(T.sem.st, 16)
        stores += 1
    elif rank == root3:
        n3 = 16 + sum(len(_common(topo, T.cores[r], [core])) for r in g3 if r != rank)
        g.scalar.wait_ge(T.sem.arr3, n3)
        g.scalar.dma_start(T.y3[:], T.land3[:]).then_inc(T.sem.st, 16)
        stores += 1
    g.wait_ge(T.sem.sent, sent)
    g.wait_ge(T.sem.st, 16 * stores)
